import numpy as np
import ml_dtypes


def mxq(x, axis, fmt="e4m3"):
    dtype, down = {"e4m3": (ml_dtypes.float8_e4m3fn, 7), "e5m2": (ml_dtypes.float8_e5m2, 14)}[fmt]
    v = np.moveaxis(np.asarray(x, np.float32).astype(ml_dtypes.bfloat16).astype(np.float64), axis, -1)
    blocks = v.reshape(v.shape[:-1] + (-1, 32))
    amax = np.abs(blocks).max(-1, keepdims=True)
    byte = np.maximum(np.where(amax > 0, np.frexp(amax)[1] - 1 + 127, 0) - down, 1)
    scale = np.exp2(byte - 127.0)
    codes = (blocks / scale).astype(np.float32).astype(dtype).astype(np.float64)
    return np.moveaxis((codes * scale).reshape(v.shape), -1, axis)


WIDE = False


def mx_kscale(k):
    if not WIDE:
        return np.ones(k)
    levels = np.array([10, -10, 5, -5, 0])
    if k % 512:
        return np.exp2(np.random.permutation(np.resize(levels, k // 32))).repeat(32)
    a = np.empty((k // 512, 16))
    for p in range(k // 512):
        a[p, :8] = np.random.permutation(np.resize(levels, 8))
        for g in range(8):
            far = levels[np.abs(levels - a[p, g]) >= 10]
            a[p, g + 8] = far[np.random.randint(len(far))]
    return np.exp2(a.ravel()).repeat(32)


def f64(x):
    return np.asarray(x).astype(np.float64)


def striped(idx):
    return np.tile(idx.reshape(-1, 16).T, (8, 1)).astype(np.uint16)


def unstriped(offs):
    return offs[:16].T.reshape(-1).astype(np.int64)


def pack_weight(w):
    k, n = w.shape
    w = f64(np.asarray(w, np.float32).astype(ml_dtypes.bfloat16)).reshape(k // 32, 32, n)
    amax = np.abs(w).max(1)
    byte = np.clip(np.where(amax > 0, np.frexp(amax)[1] - 1 + 127 - 7, 1), 1, 254)
    scaled = (w * np.exp2(127.0 - byte)[:, None, :]).reshape(k, n).astype(np.float32)
    words = np.ascontiguousarray(scaled.reshape(k // 512, 128, 4, n).transpose(0, 1, 3, 2)).astype(ml_dtypes.float8_e4m3fn).view(np.uint8)
    return words, np.ascontiguousarray(byte.astype(np.uint8).reshape(k // 512, 16, n))


def unpack_weight(words, scales):
    g, p, n, _ = words.shape
    vals = np.ascontiguousarray(words).view(ml_dtypes.float8_e4m3fn).astype(np.float64) * np.repeat(np.exp2(scales.astype(np.float64) - 127.0), 8, axis=1)[..., None]
    return vals.transpose(0, 1, 3, 2).reshape(g * 512, n)


def silu(v):
    return v / (1.0 + np.exp(-np.maximum(v, -700.0)))


K, T, S, V, H, N = 512, 2048, 1024, 512, 512, 256


def setup_inputs():
    n = np.random.standard_normal
    s = mx_kscale(K)[:, None]
    u = mx_kscale(H)
    packed_w2 = pack_weight(n((H, N)) / np.sqrt(3 * H) / u[:, None])
    packed_w3 = pack_weight(n((H, N)) / np.sqrt(3 * H) / u[:, None])
    packed_w4 = pack_weight(n((H, N)) / np.sqrt(3 * H) / u[:, None])
    return {
        "xT": (n((K, T)) * s).astype(np.float32),
        "w1": (n((K, H)) / np.sqrt(K) / s * u).astype(np.float32),
        "w2_words": packed_w2[0],
        "w2_scales": packed_w2[1],
        "w3_words": packed_w3[0],
        "w3_scales": packed_w3[1],
        "w4_words": packed_w4[0],
        "w4_scales": packed_w4[1],
        "offs": striped(np.random.permutation(T)[:S]),
        "pos1": striped(np.random.permutation(S)[:V]),
        "pos2": striped(np.random.permutation(S)[:V]),
        "pos3": striped(np.random.permutation(S)[:V]),
        "pos4": striped(np.random.permutation(S)[:V]),
    }


def reference(xT, w1, w2_words, w2_scales, w3_words, w3_scales, w4_words, w4_scales, offs, pos1, pos2, pos3, pos4):
    xq = mxq(f64(xT)[:, unstriped(offs)], 0, "e4m3")
    h = silu(mxq(f64(w1), 0, "e4m3").T @ xq)
    g0 = h[:, unstriped(pos1)]
    g1 = h[:, unstriped(pos2)]
    g2 = h[:, unstriped(pos3)]
    g3 = h[:, unstriped(pos4)]
    z1 = (g0 + g1 + g2 + g3) / 4
    z2 = np.maximum(np.maximum(np.maximum(g0, g1), g2), g3)
    z3 = np.minimum(np.minimum(np.minimum(g0, g1), g2), g3)
    return unpack_weight(w2_words, w2_scales).T @ mxq(z1, 0, "e4m3") + unpack_weight(w3_words, w3_scales).T @ mxq(z2, 0, "e4m3") + unpack_weight(w4_words, w4_scales).T @ mxq(z3, 0, "e4m3")

@@ -1,0 +1,233 @@
+from contextlib import ExitStack
+
+import concourse.mybir as mybir
+from concourse.masks import make_identity
+
+K, T, S, V, H, N = 512, 2048, 1024, 512, 512, 256
+FLOPS = 2 * K * H * S + 3 * 2 * H * N * V
+
+F32 = mybir.dt.float32
+BF16 = mybir.dt.bfloat16
+I32 = mybir.dt.int32
+U32 = mybir.dt.uint32
+U16 = mybir.dt.uint16
+U8 = mybir.dt.uint8
+FP8X4 = mybir.dt.float8_e4m3fn_x4
+ACT = mybir.ActivationFunctionType
+ALU = mybir.AluOpType
+
+P = 128
+PACK = 4
+BANK = 512
+X_CHUNK = 512
+S_HALF = S // 2
+V_HALF = V // 2
+DEG = 4
+LAST_SPLIT = 320
+
+
+def tile_picked_pna_silu_e_kernel(
+    tc, xT, w1, w2_words, w2_scales, w3_words, w3_scales, w4_words, w4_scales, offs, pos1, pos2, pos3, pos4, out
+):
+    nc = tc.nc
+    with ExitStack() as ctx:
+        keep = ctx.enter_context(tc.tile_pool(name="keep", bufs=1))
+        ring = ctx.enter_context(tc.tile_pool(name="ring", bufs=2))
+        psum = ctx.enter_context(tc.psum_pool(name="psum", bufs=4))
+
+        def quantize(name, values):
+            width = values.shape[1] // PACK
+            codes = keep.tile([P, width], U32, name=name + "_codes", align_bytes=64)
+            scales = keep.tile([P, width], U8, name=name + "_scales", align_bytes=64)
+            nc.vector.quantize_mx(out=codes[:].bitcast(FP8X4), scales=scales[:], in_=values)
+            return codes, scales
+
+        x_rows = xT.rearrange("(p u e) t -> p u e t", u=2, e=2)
+        chunks = T // X_CHUNK
+        offs_sb = keep.tile([P, S // 16], U16, name="offs_sb")
+        x_raw = {}
+        for u in range(2):
+            for c in range(chunks):
+                x_raw[u, c] = keep.tile([P, 2, X_CHUNK], F32, name="x_raw_%d_%d" % (u, c))
+                nc.sync.dma_start(out=x_raw[u, c][:], in_=x_rows[:, u, :, c * X_CHUNK : (c + 1) * X_CHUNK])
+                if (u, c) == (0, 0):
+                    nc.sync.dma_start(offs_sb[:], offs)
+        w1_raw = keep.tile([P, PACK, H], F32, name="w1_raw")
+        nc.sync.dma_start(out=w1_raw[:], in_=w1.rearrange("(p j) c -> p j c", j=PACK))
+        pos_sb = []
+        for d, pos in enumerate((pos1, pos2, pos3, pos4)):
+            pos_sb.append(keep.tile([P, V // 16], U16, name="pos_sb_%d" % d))
+            nc.sync.dma_start(pos_sb[d][:], pos)
+
+        wz_codes, wz_scales = [], []
+        for a, (words, scales) in enumerate(((w2_words, w2_scales), (w3_words, w3_scales), (w4_words, w4_scales))):
+            wz_codes.append(keep.tile([P, N], U32, name="wz_codes_%d" % a, align_bytes=64))
+            wz_scales.append(keep.tile([P, N], U8, name="wz_scales_%d" % a, align_bytes=64))
+            nc.sync.dma_start(
+                out=wz_codes[a][:].bitcast(I32), in_=words[0].rearrange("p n t -> p (n t)").bitcast(I32)
+            )
+            nc.vector.memset(wz_scales[a][:].bitcast(I32), 0)
+            for q in range(4):
+                nc.sync.dma_start(
+                    out=wz_scales[a][32 * q : 32 * q + 4, :].bitcast(I32),
+                    in_=scales[0, 4 * q : 4 * q + 4, :].bitcast(I32),
+                )
+
+        ident = keep.tile([P, P], F32, name="ident")
+        make_identity(nc, ident[:])
+
+        x_pairs = [keep.tile([P, T, 2], BF16, name="x_pairs_%d" % u) for u in range(2)]
+        x_picked = keep.tile([P, 2, S], U32, name="x_picked")
+
+        def round_pairs(copy, u, c, lo, hi):
+            copy(
+                x_pairs[u][:, c * X_CHUNK + lo : c * X_CHUNK + hi, :],
+                x_raw[u, c][:, :, lo:hi].rearrange("p e t -> p t e"),
+            )
+
+        def pair_words(u):
+            return x_pairs[u][:].rearrange("p t e -> p (t e)").bitcast(U32)
+
+        for c in range(chunks):
+            round_pairs(nc.vector.tensor_copy, 0, c, 0, X_CHUNK)
+        nc.vector.tensor_copy(x_picked[:, 0, :], pair_words(0).indirect(offs_sb[:]))
+        round_pairs(nc.scalar.copy, 1, 0, 0, X_CHUNK)
+        round_pairs(nc.scalar.copy, 1, 1, 0, X_CHUNK)
+        round_pairs(nc.vector.tensor_copy, 1, 2, 0, X_CHUNK)
+        round_pairs(nc.vector.tensor_copy, 1, 3, 0, LAST_SPLIT)
+        round_pairs(nc.scalar.copy, 1, 3, LAST_SPLIT, X_CHUNK)
+
+        x_woven = []
+        for half in range(2):
+            cols = slice(half * S_HALF, (half + 1) * S_HALF)
+            entries = offs_sb[:, half * S_HALF // 16 : (half + 1) * S_HALF // 16]
+            nc.vector.tensor_copy(x_picked[:, 1, cols], pair_words(1).indirect(entries))
+            x_woven.append(keep.tile([P, S_HALF, 2], U32, name="x_woven_%d" % half, align_bytes=64))
+            nc.scalar.copy(x_woven[half][:], x_picked[:, :, cols].rearrange("p u s -> p s u"))
+
+        def quantize_x(half):
+            return quantize("x_%d" % half, x_woven[half][:].rearrange("p s u -> p (s u)").bitcast(BF16))
+
+        def deal_w1(copy, t):
+            dealt = keep.tile([P, P, PACK], BF16, name="w1_dealt_%d" % t, align_bytes=64)
+            copy(dealt[:], w1_raw[:].rearrange("p j (m t) -> p t m j", t=PACK)[:, t, :, :])
+            return dealt
+
+        def quantize_w1(t):
+            return quantize("w1_%d" % t, w1_dealt[t][:].rearrange("p m j -> p (m j)"))
+
+        xq, wq, w1_dealt = {}, {}, {}
+        w1_dealt[0] = deal_w1(nc.vector.tensor_copy, 0)
+        xq[0] = quantize_x(0)
+        wq[0] = quantize_w1(0)
+        xq[1] = quantize_x(1)
+        w1_dealt[1] = deal_w1(nc.scalar.copy, 1)
+        w1_dealt[2] = deal_w1(nc.vector.tensor_copy, 2)
+        wq[1] = quantize_w1(1)
+        w1_dealt[3] = deal_w1(nc.vector.tensor_copy, 3)
+        wq[2] = quantize_w1(2)
+        wq[3] = quantize_w1(3)
+
+        h = keep.tile([P, PACK * S], F32, name="h")
+        for t in range(PACK):
+            for half in range(2):
+                acc = psum.tile([P, BANK], F32, name="acc", tag="mm")
+                nc.tensor.matmul_mx(
+                    out=acc[:],
+                    lhsT=wq[t][0][:].bitcast(FP8X4),
+                    lhsT_scale=wq[t][1][:],
+                    rhs=xq[half][0][:].bitcast(FP8X4),
+                    rhs_scale=xq[half][1][:],
+                    start=True,
+                    stop=True,
+                )
+                lo = t * S + half * S_HALF
+                nc.scalar.activation(h[:, lo : lo + S_HALF], acc[:], ACT.Silu)
+
+        sums = [psum.tile([P, PACK, P], F32, name="sums_%d" % b, tag="sums") for b in range(V // P)]
+        g16 = []
+        for d in range(DEG):
+            g = ring.tile([P, PACK, V], F32, name="g")
+            for t in range(PACK):
+                end = PACK * S if d == 1 else (t + 1) * S
+                nc.vector.tensor_copy(g[:, t, :], h[:, t * S : end].indirect(pos_sb[d][:]))
+                for b in range(V // P):
+                    nc.tensor.matmul(
+                        sums[b][:, t, :],
+                        g[:, t, b * P : (b + 1) * P],
+                        ident[:],
+                        start=(d == 0 and t == 0),
+                        stop=(d == DEG - 1 and t == PACK - 1),
+                        is_transpose=True,
+                    )
+            g16.append(keep.tile([P, V, PACK], BF16, name="g16_%d" % d))
+            nc.scalar.copy(
+                g16[d][:].rearrange("p (c i) t -> p c t i", i=4),
+                g[:].rearrange("p t (c i) -> p c t i", i=4),
+            )
+
+        flat = [g16[d][:].rearrange("p v t -> p (v t)") for d in range(DEG)]
+        running = {}
+        for name, op in (("max", ALU.max), ("min", ALU.min)):
+            running[name, 1] = keep.tile([P, V * PACK], BF16, name=name + "_01")
+            nc.vector.tensor_tensor(running[name, 1][:], flat[0], flat[1], op)
+        for name, op in (("max", ALU.max), ("min", ALU.min)):
+            running[name, 2] = keep.tile([P, V * PACK], BF16, name=name + "_012")
+            nc.vector.tensor_tensor(running[name, 2][:], running[name, 1][:], flat[2], op)
+
+        def extreme(name, op, half):
+            cols = slice(half * V_HALF * PACK, (half + 1) * V_HALF * PACK)
+            z = keep.tile([P, V_HALF * PACK], BF16, name="z_%s_%d" % (name, half), align_bytes=64)
+            nc.vector.tensor_tensor(z[:], running[name, 2][:, cols], flat[3][:, cols], op)
+            return z
+
+        def mean(half):
+            back = psum.tile([P, 2, 2, P], F32, name="back", tag="mm")
+            for i in range(2):
+                b = 2 * half + i
+                turned = keep.tile([P, 2, P, 2], BF16, name="mean_turned_%d" % b)
+                nc.scalar.activation(
+                    turned[:], sums[b][:].rearrange("v (u e) p -> v u p e", e=2), ACT.Copy, scale=1.0 / DEG
+                )
+                words = turned[:].rearrange("v u p e -> v (u p e)").bitcast(F32)
+                for u in range(2):
+                    nc.tensor.transpose(back[:, i, u, :], words[:, u * P : (u + 1) * P], ident[:])
+            z = keep.tile([P, 2, P, 2], F32, name="z_mean_%d" % half, align_bytes=64)
+            nc.scalar.copy(z[:], back[:].rearrange("p i u v -> p i v u"))
+            return z
+
+        z_mean = [mean(0), mean(1)]
+        zq = {}
+        z_max0 = extreme("max", ALU.max, 0)
+        z_min0 = extreme("min", ALU.min, 0)
+        z_max1 = extreme("max", ALU.max, 1)
+        zq[1, 0] = quantize("z_max_0", z_max0[:])
+        z_min1 = extreme("min", ALU.min, 1)
+        zq[2, 0] = quantize("z_min_0", z_min0[:])
+        zq[0, 0] = quantize("z_mean_0", z_mean[0][:].rearrange("p i v u -> p (i v u)").bitcast(BF16))
+        zq[1, 1] = quantize("z_max_1", z_max1[:])
+        zq[2, 1] = quantize("z_min_1", z_min1[:])
+        zq[0, 1] = quantize("z_mean_1", z_mean[1][:].rearrange("p i v u -> p (i v u)").bitcast(BF16))
+
+        out_rows = out.rearrange("(a p) v -> p a v", p=P)
+        for half in range(2):
+            result = keep.tile([P, N // P, V_HALF], F32, name="result_%d" % half)
+            accs = [psum.tile([P, V_HALF], F32, name="out_acc", tag=("mm", "sums")[half]) for m in range(N // P)]
+            order = (1, 2, 0)
+            for a in order:
+                for m in range(N // P):
+                    nc.tensor.matmul_mx(
+                        out=accs[m][:],
+                        lhsT=wz_codes[a][:, m * P : (m + 1) * P].bitcast(FP8X4),
+                        lhsT_scale=wz_scales[a][:, m * P : (m + 1) * P],
+                        rhs=zq[a, half][0][:].bitcast(FP8X4),
+                        rhs_scale=zq[a, half][1][:],
+                        start=(a == order[0]),
+                        stop=(a == order[-1]),
+                    )
+            nc.scalar.copy(result[:, 0, :], accs[0][:])
+            if half == 0:
+                nc.scalar.copy(result[:, 1, :], accs[1][:])
+            else:
+                nc.vector.tensor_copy(result[:, 1, :], accs[1][:])
+            nc.sync.dma_start(out=out_rows[:, :, half * V_HALF : (half + 1) * V_HALF], in_=result[:])

@@ -35,23 +35,21 @@ def tile_picked_pna_silu_e_kernel(
         ring = ctx.enter_context(tc.tile_pool(name="ring", bufs=2))
         psum = ctx.enter_context(tc.psum_pool(name="psum", bufs=4))
 
-        def quantize(name, values):
+        def quantize(name, values, tag=None):
             width = values.shape[1] // PACK
-            codes = keep.tile([P, width], U32, name=name + "_codes", align_bytes=64)
+            codes = keep.tile([P, width], U32, name=name + "_codes", tag=tag or name + "_codes", align_bytes=64)
             scales = keep.tile([P, width], U8, name=name + "_scales", align_bytes=64)
             nc.vector.quantize_mx(out=codes[:].bitcast(FP8X4), scales=scales[:], in_=values)
             return codes, scales
 
         x_rows = xT.rearrange("(p u e) t -> p u e t", u=2, e=2)
-        chunks = T // X_CHUNK
         offs_sb = keep.tile([P, S // 16], U16, name="offs_sb")
         x_raw = {}
-        for u in range(2):
-            for c in range(chunks):
-                x_raw[u, c] = keep.tile([P, 2, X_CHUNK], F32, name="x_raw_%d_%d" % (u, c))
-                nc.sync.dma_start(out=x_raw[u, c][:], in_=x_rows[:, u, :, c * X_CHUNK : (c + 1) * X_CHUNK])
-                if (u, c) == (0, 0):
-                    nc.sync.dma_start(offs_sb[:], offs)
+        for u, lo, hi in ((0, 0, 1024), (0, 1024, 2048), (1, 0, 1024), (1, 1024, 1536), (1, 1536, 2048)):
+            x_raw[u, lo] = keep.tile([P, 2, hi - lo], F32, name="x_raw_%d_%d" % (u, lo))
+            nc.sync.dma_start(out=x_raw[u, lo][:], in_=x_rows[:, u, :, lo:hi])
+            if (u, lo) == (0, 0):
+                nc.sync.dma_start(offs_sb[:], offs)
         w1_raw = keep.tile([P, PACK, H], F32, name="w1_raw")
         nc.sync.dma_start(out=w1_raw[:], in_=w1.rearrange("(p j) c -> p j c", j=PACK))
         pos_sb = []
@@ -77,56 +75,54 @@ def tile_picked_pna_silu_e_kernel(
         make_identity(nc, ident[:])
 
         x_pairs = [keep.tile([P, T, 2], BF16, name="x_pairs_%d" % u) for u in range(2)]
-        x_picked = keep.tile([P, 2, S], U32, name="x_picked")
+        x_picked = [keep.tile([P, 2, S_HALF], U32, name="x_picked_%d" % half) for half in range(2)]
 
         def round_pairs(copy, u, c, lo, hi):
             copy(
-                x_pairs[u][:, c * X_CHUNK + lo : c * X_CHUNK + hi, :],
+                x_pairs[u][:, c + lo : c + hi, :],
                 x_raw[u, c][:, :, lo:hi].rearrange("p e t -> p t e"),
             )
 
         def pair_words(u):
             return x_pairs[u][:].rearrange("p t e -> p (t e)").bitcast(U32)
 
-        for c in range(chunks):
-            round_pairs(nc.vector.tensor_copy, 0, c, 0, X_CHUNK)
-        nc.vector.tensor_copy(x_picked[:, 0, :], pair_words(0).indirect(offs_sb[:]))
-        round_pairs(nc.scalar.copy, 1, 0, 0, X_CHUNK)
-        round_pairs(nc.scalar.copy, 1, 1, 0, X_CHUNK)
-        round_pairs(nc.vector.tensor_copy, 1, 2, 0, X_CHUNK)
-        round_pairs(nc.vector.tensor_copy, 1, 3, 0, LAST_SPLIT)
-        round_pairs(nc.scalar.copy, 1, 3, LAST_SPLIT, X_CHUNK)
+        def pick(u, half):
+            entries = offs_sb[:, half * S_HALF // 16 : (half + 1) * S_HALF // 16]
+            nc.vector.tensor_copy(x_picked[half][:, u, :], pair_words(u).indirect(entries))
+
+        round_pairs(nc.vector.tensor_copy, 0, 0, 0, 1024)
+        round_pairs(nc.vector.tensor_copy, 0, 1024, 0, 640)
+        round_pairs(nc.scalar.copy, 0, 1024, 640, 1024)
+        pick(0, 0)
+        pick(0, 1)
+        round_pairs(nc.scalar.copy, 1, 0, 0, 1024)
+        round_pairs(nc.vector.tensor_copy, 1, 1024, 0, 512)
+        round_pairs(nc.vector.tensor_copy, 1, 1536, 0, LAST_SPLIT)
+        round_pairs(nc.scalar.copy, 1, 1536, LAST_SPLIT, 512)
 
         x_woven = []
         for half in range(2):
-            cols = slice(half * S_HALF, (half + 1) * S_HALF)
-            entries = offs_sb[:, half * S_HALF // 16 : (half + 1) * S_HALF // 16]
-            nc.vector.tensor_copy(x_picked[:, 1, cols], pair_words(1).indirect(entries))
-            x_woven.append(keep.tile([P, S_HALF, 2], U32, name="x_woven_%d" % half, align_bytes=64))
-            nc.scalar.copy(x_woven[half][:], x_picked[:, :, cols].rearrange("p u s -> p s u"))
+            pick(1, half)
+            x_woven.append(keep.tile([P, S_HALF, 2], U32, name="x_woven", tag="staged_%d" % half, align_bytes=64))
+            nc.scalar.copy(x_woven[half][:], x_picked[half][:].rearrange("p u s -> p s u"))
 
-        def quantize_x(half):
-            return quantize("x_%d" % half, x_woven[half][:].rearrange("p s u -> p (s u)").bitcast(BF16))
+        def quantize_x(half, tag=None):
+            return quantize("x_%d" % half, x_woven[half][:].rearrange("p s u -> p (s u)").bitcast(BF16), tag)
 
-        def deal_w1(copy, t):
-            dealt = keep.tile([P, P, PACK], BF16, name="w1_dealt_%d" % t, align_bytes=64)
-            copy(dealt[:], w1_raw[:].rearrange("p j (m t) -> p t m j", t=PACK)[:, t, :, :])
-            return dealt
+        w1_cols = w1_raw[:].rearrange("p j (m t) -> p m t j", t=PACK)
 
-        def quantize_w1(t):
-            return quantize("w1_%d" % t, w1_dealt[t][:].rearrange("p m j -> p (m j)"))
+        def deal_w1(lo, tag):
+            dealt = keep.tile([P, 2, P, PACK], BF16, name="w1_dealt", tag=tag, align_bytes=64)
+            nc.vector.tensor_copy(dealt[:].rearrange("p t m j -> p m t j"), w1_cols[:, :, lo : lo + 2, :])
+            return dealt[:].rearrange("p t m j -> p (t m j)")
 
-        xq, wq, w1_dealt = {}, {}, {}
-        w1_dealt[0] = deal_w1(nc.vector.tensor_copy, 0)
+        xq = {}
+        w1_first = deal_w1(0, "w1_first")
         xq[0] = quantize_x(0)
-        wq[0] = quantize_w1(0)
-        xq[1] = quantize_x(1)
-        w1_dealt[1] = deal_w1(nc.scalar.copy, 1)
-        w1_dealt[2] = deal_w1(nc.vector.tensor_copy, 2)
-        wq[1] = quantize_w1(1)
-        w1_dealt[3] = deal_w1(nc.vector.tensor_copy, 3)
-        wq[2] = quantize_w1(2)
-        wq[3] = quantize_w1(3)
+        wq01 = quantize("w1_01", w1_first)
+        xq[1] = quantize_x(1, "w1_first")
+        wq23 = quantize("w1_23", deal_w1(2, "staged_1"))
+        wq = [(c[:, i * P : (i + 1) * P], s[:, i * P : (i + 1) * P]) for c, s in (wq01, wq23) for i in range(2)]
 
         h = keep.tile([P, PACK * S], F32, name="h")
         for t in range(PACK):
@@ -134,8 +130,8 @@ def tile_picked_pna_silu_e_kernel(
                 acc = psum.tile([P, BANK], F32, name="acc", tag="mm")
                 nc.tensor.matmul_mx(
                     out=acc[:],
-                    lhsT=wq[t][0][:].bitcast(FP8X4),
-                    lhsT_scale=wq[t][1][:],
+                    lhsT=wq[t][0].bitcast(FP8X4),
+                    lhsT_scale=wq[t][1],
                     rhs=xq[half][0][:].bitcast(FP8X4),
                     rhs_scale=xq[half][1][:],
                     start=True,

@@ -141,6 +141,13 @@ def tile_picked_pna_silu_e_kernel(
                 nc.scalar.activation(h[:, lo : lo + S_HALF], acc[:], ACT.Silu)
 
         sums = [psum.tile([P, PACK, P], F32, name="sums_%d" % b, tag="sums") for b in range(V // P)]
+
+        def round_neighbours(dst, src, lo, hi):
+            nc.scalar.copy(
+                dst[:, lo:hi, :].rearrange("p (c i) t -> p c t i", i=4),
+                src[:, :, lo:hi].rearrange("p t (c i) -> p c t i", i=4),
+            )
+
         g16 = []
         for d in range(DEG):
             g = ring.tile([P, PACK, V], F32, name="g")
@@ -157,10 +164,8 @@ def tile_picked_pna_silu_e_kernel(
                         is_transpose=True,
                     )
             g16.append(keep.tile([P, V, PACK], BF16, name="g16_%d" % d))
-            nc.scalar.copy(
-                g16[d][:].rearrange("p (c i) t -> p c t i", i=4),
-                g[:].rearrange("p t (c i) -> p c t i", i=4),
-            )
+            if d < DEG - 1:
+                round_neighbours(g16[d], g, 0, V)
 
         flat = [g16[d][:].rearrange("p v t -> p (v t)") for d in range(DEG)]
         running = {}
@@ -171,59 +176,72 @@ def tile_picked_pna_silu_e_kernel(
             running[name, 2] = keep.tile([P, V * PACK], BF16, name=name + "_012")
             nc.vector.tensor_tensor(running[name, 2][:], running[name, 1][:], flat[2], op)
 
-        def extreme(name, op, half):
-            cols = slice(half * V_HALF * PACK, (half + 1) * V_HALF * PACK)
-            z = keep.tile([P, V_HALF * PACK], BF16, name="z_%s_%d" % (name, half), align_bytes=64)
-            nc.vector.tensor_tensor(z[:], running[name, 2][:, cols], flat[3][:, cols], op)
-            return z
+        def extremes(lo, hi):
+            round_neighbours(g16[DEG - 1], g, lo, hi)
+            cols = slice(lo * PACK, hi * PACK)
+            z = {}
+            for name, op in (("max", ALU.max), ("min", ALU.min)):
+                z[name] = keep.tile([P, (hi - lo) * PACK], BF16, name="z_%s_%d" % (name, lo), align_bytes=64)
+                nc.vector.tensor_tensor(z[name][:], running[name, 2][:, cols], flat[DEG - 1][:, cols], op)
+            return [quantize("z_%s_%d" % (name, lo), z[name][:]) for name in ("max", "min")]
 
-        def mean(half):
-            back = psum.tile([P, 2, 2, P], F32, name="back", tag="mm")
-            for i in range(2):
-                b = 2 * half + i
+        def means():
+            backs = [psum.tile([P, 2, 2, P], F32, name="back", tag="mm") for half in range(2)]
+            for b in range(V // P):
                 turned = keep.tile([P, 2, P, 2], BF16, name="mean_turned_%d" % b)
                 nc.scalar.activation(
                     turned[:], sums[b][:].rearrange("v (u e) p -> v u p e", e=2), ACT.Copy, scale=1.0 / DEG
                 )
                 words = turned[:].rearrange("v u p e -> v (u p e)").bitcast(F32)
                 for u in range(2):
-                    nc.tensor.transpose(back[:, i, u, :], words[:, u * P : (u + 1) * P], ident[:])
-            z = keep.tile([P, 2, P, 2], F32, name="z_mean_%d" % half, align_bytes=64)
-            nc.scalar.copy(z[:], back[:].rearrange("p i u v -> p i v u"))
-            return z
+                    nc.tensor.transpose(backs[b // 2][:, b % 2, u, :], words[:, u * P : (u + 1) * P], ident[:])
+            quantized = []
+            for half in range(2):
+                z = keep.tile([P, 2, P, 2], F32, name="z_mean_%d" % half, align_bytes=64)
+                nc.scalar.copy(z[:], backs[half][:].rearrange("p i u v -> p i v u"))
+                quantized.append(quantize("z_mean_%d" % half, z[:].rearrange("p i v u -> p (i v u)").bitcast(BF16)))
+            return quantized
 
-        z_mean = [mean(0), mean(1)]
-        zq = {}
-        z_max0 = extreme("max", ALU.max, 0)
-        z_min0 = extreme("min", ALU.min, 0)
-        z_max1 = extreme("max", ALU.max, 1)
-        zq[1, 0] = quantize("z_max_0", z_max0[:])
-        z_min1 = extreme("min", ALU.min, 1)
-        zq[2, 0] = quantize("z_min_0", z_min0[:])
-        zq[0, 0] = quantize("z_mean_0", z_mean[0][:].rearrange("p i v u -> p (i v u)").bitcast(BF16))
-        zq[1, 1] = quantize("z_max_1", z_max1[:])
-        zq[2, 1] = quantize("z_min_1", z_min1[:])
-        zq[0, 1] = quantize("z_mean_1", z_mean[1][:].rearrange("p i v u -> p (i v u)").bitcast(BF16))
-
-        out_rows = out.rearrange("(a p) v -> p a v", p=P)
-        for half in range(2):
-            result = keep.tile([P, N // P, V_HALF], F32, name="result_%d" % half)
-            accs = [psum.tile([P, V_HALF], F32, name="out_acc", tag=("mm", "sums")[half]) for m in range(N // P)]
-            order = (1, 2, 0)
-            for a in order:
+        def second_product(lo, hi, passes, tag, last):
+            accs = [psum.tile([P, hi - lo], F32, name="out_acc", tag=tag) for m in range(N // P)]
+            for i, (a, codes, scales) in enumerate(passes):
                 for m in range(N // P):
                     nc.tensor.matmul_mx(
                         out=accs[m][:],
                         lhsT=wz_codes[a][:, m * P : (m + 1) * P].bitcast(FP8X4),
                         lhsT_scale=wz_scales[a][:, m * P : (m + 1) * P],
-                        rhs=zq[a, half][0][:].bitcast(FP8X4),
-                        rhs_scale=zq[a, half][1][:],
-                        start=(a == order[0]),
-                        stop=(a == order[-1]),
+                        rhs=codes.bitcast(FP8X4),
+                        rhs_scale=scales,
+                        start=(i == 0),
+                        stop=(i == len(passes) - 1),
                     )
-            nc.scalar.copy(result[:, 0, :], accs[0][:])
-            if half == 0:
-                nc.scalar.copy(result[:, 1, :], accs[1][:])
+            if last:
+                for m, (copy, queue) in enumerate(((nc.scalar.copy, nc.scalar), (nc.vector.tensor_copy, nc.sync))):
+                    result = keep.tile([P, hi - lo], F32, name="result_%d_%d" % (lo, m))
+                    copy(result[:], accs[m][:])
+                    queue.dma_start(out=out[m * P : (m + 1) * P, lo:hi], in_=result[:])
             else:
-                nc.vector.tensor_copy(result[:, 1, :], accs[1][:])
-            nc.sync.dma_start(out=out_rows[:, :, half * V_HALF : (half + 1) * V_HALF], in_=result[:])
+                result = keep.tile([P, N // P, hi - lo], F32, name="result_%d" % lo)
+                for m in range(N // P):
+                    nc.scalar.copy(result[:, m, :], accs[m][:])
+                nc.sync.dma_start(out=out.rearrange("(a p) v -> p a v", p=P)[:, :, lo:hi], in_=result[:])
+
+        z_max, z_min = extremes(0, V_HALF)
+        z_mean = means()
+        second_product(
+            0,
+            V_HALF,
+            [(1, z_max[0][:], z_max[1][:]), (2, z_min[0][:], z_min[1][:]), (0, z_mean[0][0][:], z_mean[0][1][:])],
+            "mm",
+            False,
+        )
+        for lo in range(V_HALF, V, P):
+            z_max, z_min = extremes(lo, lo + P)
+            cols = slice(lo - V_HALF, lo - V_HALF + P)
+            second_product(
+                lo,
+                lo + P,
+                [(0, z_mean[1][0][:, cols], z_mean[1][1][:, cols]), (1, z_max[0][:], z_max[1][:]), (2, z_min[0][:], z_min[1][:])],
+                "sums",
+                lo + P == V,
+            )

from contextlib import ExitStack

import concourse.mybir as mybir
from concourse.masks import make_identity

K, T, S, V, H, N = 512, 2048, 1024, 512, 512, 256
FLOPS = 2 * K * H * S + 3 * 2 * H * N * V

F32 = mybir.dt.float32
BF16 = mybir.dt.bfloat16
I32 = mybir.dt.int32
U32 = mybir.dt.uint32
U16 = mybir.dt.uint16
U8 = mybir.dt.uint8
FP8X4 = mybir.dt.float8_e4m3fn_x4
ACT = mybir.ActivationFunctionType
ALU = mybir.AluOpType

P = 128
PACK = 4
BANK = 512
X_CHUNK = 512
S_HALF = S // 2
V_HALF = V // 2
DEG = 4
LAST_SPLIT = 320


def tile_picked_pna_silu_e_kernel(
    tc, xT, w1, w2_words, w2_scales, w3_words, w3_scales, w4_words, w4_scales, offs, pos1, pos2, pos3, pos4, out
):
    nc = tc.nc
    with ExitStack() as ctx:
        keep = ctx.enter_context(tc.tile_pool(name="keep", bufs=1))
        ring = ctx.enter_context(tc.tile_pool(name="ring", bufs=2))
        psum = ctx.enter_context(tc.psum_pool(name="psum", bufs=4))

        def quantize(name, values, tag=None):
            width = values.shape[1] // PACK
            codes = keep.tile([P, width], U32, name=name + "_codes", tag=tag or name + "_codes", align_bytes=64)
            scales = keep.tile([P, width], U8, name=name + "_scales", align_bytes=64)
            nc.vector.quantize_mx(out=codes[:].bitcast(FP8X4), scales=scales[:], in_=values)
            return codes, scales

        x_rows = xT.rearrange("(p u e) t -> p u e t", u=2, e=2)
        offs_sb = keep.tile([P, S // 16], U16, name="offs_sb")
        x_raw = {}
        for u, lo, hi in ((0, 0, 1024), (0, 1024, 2048), (1, 0, 1024), (1, 1024, 1536), (1, 1536, 2048)):
            x_raw[u, lo] = keep.tile([P, 2, hi - lo], F32, name="x_raw_%d_%d" % (u, lo))
            nc.sync.dma_start(out=x_raw[u, lo][:], in_=x_rows[:, u, :, lo:hi])
            if (u, lo) == (0, 0):
                nc.sync.dma_start(offs_sb[:], offs)
        w1_raw = keep.tile([P, PACK, H], F32, name="w1_raw")
        nc.sync.dma_start(out=w1_raw[:], in_=w1.rearrange("(p j) c -> p j c", j=PACK))
        pos_sb = []
        for d, pos in enumerate((pos1, pos2, pos3, pos4)):
            pos_sb.append(keep.tile([P, V // 16], U16, name="pos_sb_%d" % d))
            nc.sync.dma_start(pos_sb[d][:], pos)

        wz_codes, wz_scales = [], []
        for a, (words, scales) in enumerate(((w2_words, w2_scales), (w3_words, w3_scales), (w4_words, w4_scales))):
            wz_codes.append(keep.tile([P, N], U32, name="wz_codes_%d" % a, align_bytes=64))
            wz_scales.append(keep.tile([P, N], U8, name="wz_scales_%d" % a, align_bytes=64))
            nc.sync.dma_start(
                out=wz_codes[a][:].bitcast(I32), in_=words[0].rearrange("p n t -> p (n t)").bitcast(I32)
            )
            nc.vector.memset(wz_scales[a][:].bitcast(I32), 0)
            for q in range(4):
                nc.sync.dma_start(
                    out=wz_scales[a][32 * q : 32 * q + 4, :].bitcast(I32),
                    in_=scales[0, 4 * q : 4 * q + 4, :].bitcast(I32),
                )

        ident = keep.tile([P, P], F32, name="ident")
        make_identity(nc, ident[:])

        x_pairs = [keep.tile([P, T, 2], BF16, name="x_pairs_%d" % u) for u in range(2)]
        x_picked = [keep.tile([P, 2, S_HALF], U32, name="x_picked_%d" % half) for half in range(2)]

        def round_pairs(copy, u, c, lo, hi):
            copy(
                x_pairs[u][:, c + lo : c + hi, :],
                x_raw[u, c][:, :, lo:hi].rearrange("p e t -> p t e"),
            )

        def pair_words(u):
            return x_pairs[u][:].rearrange("p t e -> p (t e)").bitcast(U32)

        def pick(u, half):
            entries = offs_sb[:, half * S_HALF // 16 : (half + 1) * S_HALF // 16]
            nc.vector.tensor_copy(x_picked[half][:, u, :], pair_words(u).indirect(entries))

        round_pairs(nc.vector.tensor_copy, 0, 0, 0, 1024)
        round_pairs(nc.vector.tensor_copy, 0, 1024, 0, 640)
        round_pairs(nc.scalar.copy, 0, 1024, 640, 1024)
        pick(0, 0)
        pick(0, 1)
        round_pairs(nc.scalar.copy, 1, 0, 0, 1024)
        round_pairs(nc.vector.tensor_copy, 1, 1024, 0, 512)
        round_pairs(nc.vector.tensor_copy, 1, 1536, 0, LAST_SPLIT)
        round_pairs(nc.scalar.copy, 1, 1536, LAST_SPLIT, 512)

        x_woven = []
        for half in range(2):
            pick(1, half)
            x_woven.append(keep.tile([P, S_HALF, 2], U32, name="x_woven", tag="staged_%d" % half, align_bytes=64))
            nc.scalar.copy(x_woven[half][:], x_picked[half][:].rearrange("p u s -> p s u"))

        def quantize_x(half, tag=None):
            return quantize("x_%d" % half, x_woven[half][:].rearrange("p s u -> p (s u)").bitcast(BF16), tag)

        w1_cols = w1_raw[:].rearrange("p j (m t) -> p m t j", t=PACK)

        def deal_w1(lo, tag):
            dealt = keep.tile([P, 2, P, PACK], BF16, name="w1_dealt", tag=tag, align_bytes=64)
            nc.vector.tensor_copy(dealt[:].rearrange("p t m j -> p m t j"), w1_cols[:, :, lo : lo + 2, :])
            return dealt[:].rearrange("p t m j -> p (t m j)")

        xq = {}
        w1_first = deal_w1(0, "w1_first")
        xq[0] = quantize_x(0)
        wq01 = quantize("w1_01", w1_first)
        xq[1] = quantize_x(1, "w1_first")
        wq23 = quantize("w1_23", deal_w1(2, "staged_1"))
        wq = [(c[:, i * P : (i + 1) * P], s[:, i * P : (i + 1) * P]) for c, s in (wq01, wq23) for i in range(2)]

        h = keep.tile([P, PACK * S], F32, name="h")
        for t in range(PACK):
            for half in range(2):
                acc = psum.tile([P, BANK], F32, name="acc", tag="mm")
                nc.tensor.matmul_mx(
                    out=acc[:],
                    lhsT=wq[t][0].bitcast(FP8X4),
                    lhsT_scale=wq[t][1],
                    rhs=xq[half][0][:].bitcast(FP8X4),
                    rhs_scale=xq[half][1][:],
                    start=True,
                    stop=True,
                )
                lo = t * S + half * S_HALF
                nc.scalar.activation(h[:, lo : lo + S_HALF], acc[:], ACT.Silu)

        sums = [psum.tile([P, PACK, P], F32, name="sums_%d" % b, tag="sums") for b in range(V // P)]

        def round_neighbours(dst, src, lo, hi):
            nc.scalar.copy(
                dst[:, lo:hi, :].rearrange("p (c i) t -> p c t i", i=4),
                src[:, :, lo:hi].rearrange("p t (c i) -> p c t i", i=4),
            )

        g16 = []
        for d in range(DEG):
            g = ring.tile([P, PACK, V], F32, name="g")
            for t in range(PACK):
                end = PACK * S if d == 1 else (t + 1) * S
                nc.vector.tensor_copy(g[:, t, :], h[:, t * S : end].indirect(pos_sb[d][:]))
                for b in range(V // P):
                    nc.tensor.matmul(
                        sums[b][:, t, :],
                        g[:, t, b * P : (b + 1) * P],
                        ident[:],
                        start=(d == 0 and t == 0),
                        stop=(d == DEG - 1 and t == PACK - 1),
                        is_transpose=True,
                    )
            g16.append(keep.tile([P, V, PACK], BF16, name="g16_%d" % d))
            if d < DEG - 1:
                round_neighbours(g16[d], g, 0, V)

        flat = [g16[d][:].rearrange("p v t -> p (v t)") for d in range(DEG)]
        running = {}
        for name, op in (("max", ALU.max), ("min", ALU.min)):
            running[name, 1] = keep.tile([P, V * PACK], BF16, name=name + "_01")
            nc.vector.tensor_tensor(running[name, 1][:], flat[0], flat[1], op)
        for name, op in (("max", ALU.max), ("min", ALU.min)):
            running[name, 2] = keep.tile([P, V * PACK], BF16, name=name + "_012")
            nc.vector.tensor_tensor(running[name, 2][:], running[name, 1][:], flat[2], op)

        def extremes(lo, hi):
            round_neighbours(g16[DEG - 1], g, lo, hi)
            cols = slice(lo * PACK, hi * PACK)
            z = {}
            for name, op in (("max", ALU.max), ("min", ALU.min)):
                z[name] = keep.tile([P, (hi - lo) * PACK], BF16, name="z_%s_%d" % (name, lo), align_bytes=64)
                nc.vector.tensor_tensor(z[name][:], running[name, 2][:, cols], flat[DEG - 1][:, cols], op)
            return [quantize("z_%s_%d" % (name, lo), z[name][:]) for name in ("max", "min")]

        def means():
            backs = [psum.tile([P, 2, 2, P], F32, name="back", tag="mm") for half in range(2)]
            for b in range(V // P):
                turned = keep.tile([P, 2, P, 2], BF16, name="mean_turned_%d" % b)
                nc.scalar.activation(
                    turned[:], sums[b][:].rearrange("v (u e) p -> v u p e", e=2), ACT.Copy, scale=1.0 / DEG
                )
                words = turned[:].rearrange("v u p e -> v (u p e)").bitcast(F32)
                for u in range(2):
                    nc.tensor.transpose(backs[b // 2][:, b % 2, u, :], words[:, u * P : (u + 1) * P], ident[:])
            quantized = []
            for half in range(2):
                z = keep.tile([P, 2, P, 2], F32, name="z_mean_%d" % half, align_bytes=64)
                nc.scalar.copy(z[:], backs[half][:].rearrange("p i u v -> p i v u"))
                quantized.append(quantize("z_mean_%d" % half, z[:].rearrange("p i v u -> p (i v u)").bitcast(BF16)))
            return quantized

        def second_product(lo, hi, passes, tag, last):
            accs = [psum.tile([P, hi - lo], F32, name="out_acc", tag=tag) for m in range(N // P)]
            for i, (a, codes, scales) in enumerate(passes):
                for m in range(N // P):
                    nc.tensor.matmul_mx(
                        out=accs[m][:],
                        lhsT=wz_codes[a][:, m * P : (m + 1) * P].bitcast(FP8X4),
                        lhsT_scale=wz_scales[a][:, m * P : (m + 1) * P],
                        rhs=codes.bitcast(FP8X4),
                        rhs_scale=scales,
                        start=(i == 0),
                        stop=(i == len(passes) - 1),
                    )
            if last:
                for m, (copy, queue) in enumerate(((nc.scalar.copy, nc.scalar), (nc.vector.tensor_copy, nc.sync))):
                    result = keep.tile([P, hi - lo], F32, name="result_%d_%d" % (lo, m))
                    copy(result[:], accs[m][:])
                    queue.dma_start(out=out[m * P : (m + 1) * P, lo:hi], in_=result[:])
            else:
                result = keep.tile([P, N // P, hi - lo], F32, name="result_%d" % lo)
                for m in range(N // P):
                    nc.scalar.copy(result[:, m, :], accs[m][:])
                nc.sync.dma_start(out=out.rearrange("(a p) v -> p a v", p=P)[:, :, lo:hi], in_=result[:])

        z_max, z_min = extremes(0, V_HALF)
        z_mean = means()
        second_product(
            0,
            V_HALF,
            [(1, z_max[0][:], z_max[1][:]), (2, z_min[0][:], z_min[1][:]), (0, z_mean[0][0][:], z_mean[0][1][:])],
            "mm",
            False,
        )
        for lo in range(V_HALF, V, P):
            z_max, z_min = extremes(lo, lo + P)
            cols = slice(lo - V_HALF, lo - V_HALF + P)
            second_product(
                lo,
                lo + P,
                [(0, z_mean[1][0][:, cols], z_mean[1][1][:, cols]), (1, z_max[0][:], z_max[1][:]), (2, z_min[0][:], z_min[1][:])],
                "sums",
                lo + P == V,
            )
